import numpy as np
import ml_dtypes


def mxq(x, axis, fmt="e4m3"):
    dtype, down = {"e4m3": (ml_dtypes.float8_e4m3fn, 7), "e5m2": (ml_dtypes.float8_e5m2, 14)}[fmt]
    v = np.moveaxis(np.asarray(x, np.float32).astype(ml_dtypes.bfloat16).astype(np.float64), axis, -1)
    blocks = v.reshape(v.shape[:-1] + (-1, 32))
    amax = np.abs(blocks).max(-1, keepdims=True)
    byte = np.maximum(np.where(amax > 0, np.frexp(amax)[1] - 1 + 127, 0) - down, 1)
    scale = np.exp2(byte - 127.0)
    codes = (blocks / scale).astype(np.float32).astype(dtype).astype(np.float64)
    return np.moveaxis((codes * scale).reshape(v.shape), -1, axis)


WIDE = False


def mx_kscale(k):
    if not WIDE:
        return np.ones(k)
    levels = np.array([10, -10, 5, -5, 0])
    if k % 512:
        return np.exp2(np.random.permutation(np.resize(levels, k // 32))).repeat(32)
    a = np.empty((k // 512, 16))
    for p in range(k // 512):
        a[p, :8] = np.random.permutation(np.resize(levels, 8))
        for g in range(8):
            far = levels[np.abs(levels - a[p, g]) >= 10]
            a[p, g + 8] = far[np.random.randint(len(far))]
    return np.exp2(a.ravel()).repeat(32)


def f64(x):
    return np.asarray(x).astype(np.float64)


def striped(idx):
    return np.tile(idx.reshape(-1, 16).T, (8, 1)).astype(np.uint16)


def unstriped(offs):
    return offs[:16].T.reshape(-1).astype(np.int64)


def striped8(idx):
    return np.concatenate([x.reshape(-1, 16).T for x in idx]).astype(np.uint16)


def runs(offs, k):
    lists = np.stack([offs[16 * r : 16 * r + 16].T.reshape(-1) for r in range(8)]).astype(np.int64)
    return lists[np.arange(k) % 512 // 64]


def pack_weight(w):
    k, n = w.shape
    w = f64(np.asarray(w, np.float32).astype(ml_dtypes.bfloat16)).reshape(k // 32, 32, n)
    amax = np.abs(w).max(1)
    byte = np.clip(np.where(amax > 0, np.frexp(amax)[1] - 1 + 127 - 7, 1), 1, 254)
    scaled = (w * np.exp2(127.0 - byte)[:, None, :]).reshape(k, n).astype(np.float32)
    words = np.ascontiguousarray(scaled.reshape(k // 512, 128, 4, n).transpose(0, 1, 3, 2)).astype(ml_dtypes.float8_e4m3fn).view(np.uint8)
    return words, np.ascontiguousarray(byte.astype(np.uint8).reshape(k // 512, 16, n))


def unpack_weight(words, scales):
    g, p, n, _ = words.shape
    vals = np.ascontiguousarray(words).view(ml_dtypes.float8_e4m3fn).astype(np.float64) * np.repeat(np.exp2(scales.astype(np.float64) - 127.0), 8, axis=1)[..., None]
    return vals.transpose(0, 1, 3, 2).reshape(g * 512, n)


def sigmoid(v):
    return 1.0 / (1.0 + np.exp(-np.maximum(v, -700.0)))


K, T, S, H, C = 512, 2048, 512, 512, 512


def setup_inputs():
    n = np.random.standard_normal
    s = mx_kscale(K)[:, None]
    packed_xT = pack_weight(n((K, T)) * s)
    return {
        "x_words": packed_xT[0],
        "x_scales": packed_xT[1],
        "w1": (n((K, H)) / np.sqrt(K) / s).astype(np.float32),
        "w2": (n((K, H)) / np.sqrt(K) / s).astype(np.float32),
        "gs": (np.random.uniform(0.5, 1.5, (K, 1)) / s).astype(np.float32),
        "offs": striped(np.random.permutation(T)[:S]),
        "two": striped(np.random.permutation(T)[:S]),
        "k0": striped8(np.stack([np.random.permutation(S) for _ in range(8)])),
        "k1": striped8(np.stack([np.random.permutation(S) for _ in range(8)])),
        "k2": striped8(np.stack([np.random.permutation(S) for _ in range(8)])),
        "k3": striped8(np.stack([np.random.permutation(S) for _ in range(8)])),
        "cand": striped(np.random.permutation(T)[:C]),
    }


def reference(x_words, x_scales, w1, w2, gs, offs, two, k0, k1, k2, k3, cand):
    x_cand = unpack_weight(x_words, x_scales)[:, unstriped(cand)]
    xq = unpack_weight(x_words, x_scales)[:, unstriped(offs)]
    y = mxq(f64(w1), 0, "e4m3").T @ xq
    b = y[np.arange(H)[:, None], runs(k1, H)]
    x_two = unpack_weight(x_words, x_scales)[:, unstriped(two)]
    t1 = sigmoid(mxq(f64(w2), 0, "e4m3").T @ x_two)
    c = y[np.arange(H)[:, None], runs(k2, H)]
    a = y[np.arange(H)[:, None], runs(k0, H)]
    c1 = 0.5 * (c - a)
    d = y[np.arange(H)[:, None], runs(k3, H)]
    c2 = a + 2.0 * c - (2.5 * b + 0.5 * d)
    c3 = 1.5 * (b - c) + 0.5 * (d - a)
    z = f64(gs) * (b + t1 * (c1 + t1 * (c2 + t1 * c3)))
    return 0.0625 * ((x_cand.T @ mxq(z, 0, "e4m3")))

@@ -1,0 +1,283 @@
+from contextlib import ExitStack
+
+import concourse.mybir as mybir
+from concourse.masks import make_identity
+
+K, T, S = 512, 2048, 512
+FLOPS = 3 * 2 * K * S * S
+
+F32 = mybir.dt.float32
+BF16 = mybir.dt.bfloat16
+I32 = mybir.dt.int32
+U32 = mybir.dt.uint32
+U16 = mybir.dt.uint16
+U8 = mybir.dt.uint8
+FP8X4 = mybir.dt.float8_e4m3fn_x4
+ACT = mybir.ActivationFunctionType
+ALU = mybir.AluOpType
+
+P = 128
+PACK = 4
+BLOCKS = S // P
+LIST_COLS = P // 16
+SUM_BANKS = 6
+
+
+def tile_picked_catmull_none_p_kernel(
+    tc, x_words, x_scales, w1, w2, gs, offs, two, k0, k1, k2, k3, cand, out
+):
+    nc = tc.nc
+    with ExitStack() as ctx:
+        keep = ctx.enter_context(tc.tile_pool(name="keep", bufs=1))
+        psum = ctx.enter_context(tc.psum_pool(name="psum", bufs=1))
+        banks = [psum.tile([P, S], F32, name=f"bank{n}") for n in range(8)]
+        z_bank, out_bank = banks[SUM_BANKS:]
+
+        def load_list(name, src):
+            tile = keep.tile([P, S // 16], U16, name=name)
+            nc.sync.dma_start(tile[:], src)
+            return tile
+
+        table_scales = keep.tile([P, T], U8, align_bytes=64)
+        nc.gpsimd.memset(table_scales[:].bitcast(I32), 0)
+        for q in range(4):
+            nc.scalar.dma_start(
+                table_scales[32 * q : 32 * q + 4, :].bitcast(I32), x_scales[0, 4 * q : 4 * q + 4, :].bitcast(I32)
+            )
+        offs_l = load_list("offs_l", offs)
+        two_l = load_list("two_l", two)
+        cand_l = load_list("cand_l", cand)
+        w1_rows = w1.rearrange("(p j) c -> p j c", j=PACK)
+        w1_raw = []
+        for h in range(2):
+            raw = keep.tile([P, PACK, S // 2], F32, name=f"w1_raw{h}", tag=f"raw{h}")
+            nc.sync.dma_start(raw[:], w1_rows[:, :, h * (S // 2) : (h + 1) * (S // 2)])
+            w1_raw.append(raw)
+        table_words = keep.tile([P, T], U32, align_bytes=64)
+        nc.sync.dma_start(table_words[:].bitcast(I32), x_words[0].rearrange("p n t -> p (n t)").bitcast(I32))
+        gains = keep.tile([P, PACK], F32)
+        nc.sync.dma_start(gains[:], gs.rearrange("(p t) o -> p (t o)", t=PACK))
+        k1_l = load_list("k1_l", k1)
+        k2_l = load_list("k2_l", k2)
+        k0_l = load_list("k0_l", k0)
+        k3_l = load_list("k3_l", k3)
+
+        ident = keep.tile([P, P], F32)
+        make_identity(nc, ident[:])
+
+        def pick_scales(name, lst):
+            tile = keep.tile([P, S], U8, name=name, align_bytes=64)
+            nc.vector.tensor_copy(tile[:], table_scales[:].indirect(lst[:]))
+            return tile
+
+        def pick_words(name, lst):
+            tile = keep.tile([P, S], U32, name=name, align_bytes=64)
+            nc.vector.tensor_copy(tile[:], table_words[:].indirect(lst[:]))
+            return tile
+
+        offs_scales = pick_scales("offs_scales", offs_l)
+        two_scales = pick_scales("two_scales", two_l)
+        cand_scales = pick_scales("cand_scales", cand_l)
+        offs_words = pick_words("offs_words", offs_l)
+        two_words = pick_words("two_words", two_l)
+        cand_words = pick_words("cand_words", cand_l)
+
+        w1_bf = keep.tile([P, PACK * S], BF16, align_bytes=64)
+        w1_dst = w1_bf[:].rearrange("p (t m j) -> p m j t", t=PACK, j=PACK)
+        half = P // 2
+        for h in range(2):
+            nc.scalar.activation(
+                w1_dst[:, h * half : (h + 1) * half], w1_raw[h][:].rearrange("p j (m t) -> p m j t", t=PACK), ACT.Copy
+            )
+        w1_codes = keep.tile([P, S], U32, align_bytes=64)
+        w1_scales = keep.tile([P, S], U8, align_bytes=64)
+        nc.vector.quantize_mx(w1_codes[:].bitcast(FP8X4), w1_scales[:], w1_bf[:])
+        knots = []
+        for t in range(PACK):
+            cols = slice(t * P, (t + 1) * P)
+            nc.tensor.matmul_mx(
+                banks[t][:],
+                lhsT=w1_codes[:, cols].bitcast(FP8X4),
+                lhsT_scale=w1_scales[:, cols],
+                rhs=offs_words[:].bitcast(FP8X4),
+                rhs_scale=offs_scales[:],
+                start=True,
+                stop=True,
+            )
+            y = keep.tile([P, S], F32, name=f"knots{t}")
+            nc.scalar.activation(y[:], banks[t][:], ACT.Copy, scale=gains[:, t : t + 1])
+            knots.append(y)
+
+        w2_raw = keep.tile([P, PACK, S], F32, tag="raw1")
+        nc.scalar.dma_start(w2_raw[:], w2.rearrange("(p j) c -> p j c", j=PACK))
+        w2_bf = keep.tile([P, PACK * S], BF16, align_bytes=64, tag="w2_bf")
+        w2_dst = w2_bf[:].rearrange("p (c j) -> p c j", j=PACK)
+        w2_src = w2_raw[:].rearrange("p j c -> p c j")
+        nc.gpsimd.tensor_scalar(w2_dst, w2_src, 1.0, 0.0, ALU.mult, ALU.add)
+        w2_codes = keep.tile([P, S], U32, align_bytes=64)
+        w2_scales = keep.tile([P, S], U8, align_bytes=64)
+        nc.vector.quantize_mx(w2_codes[:].bitcast(FP8X4), w2_scales[:], w2_bf[:])
+
+        fetched = {}
+        negated = [
+            keep.tile([P, 2 * S], F32, name="negated0"),
+            keep.tile([P, 2 * S], F32, name="negated1", align_bytes=64, tag="w2_bf"),
+        ]
+        raw = {name: keep.tile([P, S], F32, name=name) for name in ("slope_raw", "a_slope_raw")}
+
+        def window(t, lst, b):
+            return knots[t][:].indirect(lst[:, b * LIST_COLS : (b + 1) * LIST_COLS])
+
+        def new_tile(name, b):
+            if name == "neg_b":
+                tile = negated[b % 2][:, :S]
+            elif name == "neg_d":
+                tile = negated[b % 2][:, S:]
+            elif name in raw:
+                tile = raw[name][:]
+            else:
+                tile = keep.tile([P, S], F32, name=f"{name}{b}")[:]
+            fetched[name, b] = tile
+            return tile
+
+        def fetch(name, lst, b, engine, sign):
+            tile = new_tile(name, b)
+            for t in range(PACK):
+                dst = tile[:, t * P : (t + 1) * P]
+                if engine == "S":
+                    nc.scalar.activation(dst, window(t, lst, b), ACT.Copy, scale=sign)
+                elif sign == 1.0:
+                    nc.vector.tensor_copy(dst, window(t, lst, b))
+                else:
+                    nc.vector.tensor_scalar(dst, window(t, lst, b), sign, 0.0, ALU.mult, ALU.add)
+
+        def fetch_added(name, lst, b, other, how):
+            if how == "F":
+                tile = new_tile(name, b)
+                for t in range(PACK):
+                    cols = slice(t * P, (t + 1) * P)
+                    nc.vector.tensor_tensor(tile[:, cols], window(t, lst, b), fetched[other, b][:, cols], ALU.add)
+            else:
+                fetch(name + "_raw", lst, b, how, 1.0)
+                tile = new_tile(name, b)
+                nc.gpsimd.tensor_tensor(tile[:], fetched[name + "_raw", b][:], fetched[other, b][:], ALU.add)
+
+        def fetches(b):
+            fetch("neg_b", k1_l, b, "SSSS"[b], -1.0)
+            fetch_added("slope", k2_l, b, "neg_b", "VVVS"[b])
+            fetch_added("a_slope", k0_l, b, "slope", "VVSS"[b])
+            fetch("neg_d", k3_l, b, "SSSS"[b], -1.0)
+
+        def turn_sum(bank, b, terms):
+            last = (len(terms) - 1, PACK - 1)
+            for n, term in enumerate(terms):
+                for t in range(PACK):
+                    cols = slice(t * P, (t + 1) * P)
+                    nc.tensor.matmul(
+                        bank[:, cols],
+                        lhsT=fetched[term, b][:, cols],
+                        rhs=ident[:],
+                        start=((n, t) == (0, 0)),
+                        stop=((n, t) == last),
+                        is_transpose=True,
+                    )
+            return bank[:].rearrange("j (t p) -> j p t", t=PACK)
+
+        def position(b):
+            cols = slice(b * P, (b + 1) * P)
+            pos_bank = banks[4 + b]
+            nc.tensor.matmul_mx(
+                pos_bank[:],
+                lhsT=two_words[:, cols].bitcast(FP8X4),
+                lhsT_scale=two_scales[:, cols],
+                rhs=w2_codes[:].bitcast(FP8X4),
+                rhs_scale=w2_scales[:],
+                start=True,
+                stop=True,
+            )
+            pos = keep.tile([P, S], F32, name=f"pos{b}")
+            nc.scalar.activation(pos[:], pos_bank[:], ACT.Sigmoid)
+            return pos
+
+        def turned_sums(b):
+            sums = [banks[(4 * b + n) % SUM_BANKS] for n in range(4)]
+            cubic = turn_sum(sums[0], b, ["neg_d", "slope", "slope", "a_slope"] if b + 1 < BLOCKS else ["slope", "slope", "a_slope", "neg_d"])
+            bend = turn_sum(sums[1], b, ["neg_b", "a_slope"])
+            slope = turn_sum(sums[2], b, ["slope"])
+            neg_b = turn_sum(sums[3], b, ["neg_b"])
+            return cubic, bend, slope, neg_b
+
+        def curve(b, pos, sums):
+            cubic, bend, slope, neg_b = sums
+            z_rows = keep.tile([P, S], BF16, name=f"z_rows{b}")
+            parts = 2
+            width = P // parts
+            chains = []
+            for h in range(parts):
+                rows = slice(h * width, (h + 1) * width)
+                acc = [keep.tile([P, width, PACK], F32, name=f"acc{n}_{h}_{b}") for n in range(2)]
+                pos_h = pos[:].rearrange("j (p t) -> j p t", t=PACK)[:, rows]
+                z_h = z_rows[:].rearrange("j (p t) -> j p t", t=PACK)[:, rows]
+                chains.append((rows, acc[0][:], acc[1][:], pos_h, z_h))
+            for rows, u, v, pos_h, z_h in chains:
+                nc.vector.scalar_tensor_tensor(u, cubic[:, rows], 0.5, pos_h, ALU.mult, ALU.mult)
+            for rows, u, v, pos_h, z_h in chains:
+                nc.vector.scalar_tensor_tensor(v, bend[:, rows], -0.5, u, ALU.mult, ALU.add)
+            for rows, u, v, pos_h, z_h in chains:
+                nc.vector.scalar_tensor_tensor(u, pos_h, 1.0, v, ALU.subtract, ALU.mult)
+            for rows, u, v, pos_h, z_h in chains:
+                nc.vector.tensor_tensor(v, slope[:, rows], u, ALU.subtract)
+            for rows, u, v, pos_h, z_h in chains:
+                (nc.gpsimd if "VVVV"[b] == "G" else nc.vector).tensor_tensor(u, v, pos_h, ALU.mult)
+            for rows, u, v, pos_h, z_h in chains:
+                nc.vector.tensor_tensor(z_h, u, neg_b[:, rows], ALU.subtract)
+            return z_rows
+
+        out_blocks = out.rearrange("(c p) n -> p c n", p=P)
+
+        def score(b, z_rows):
+            words = z_rows[:].bitcast(F32)
+            for u in range(2):
+                nc.tensor.transpose(z_bank[:, u * P : (u + 1) * P], words[:, u : 2 * P : 2], ident[:])
+            z_bf = keep.tile([P, PACK * P], BF16, name=f"z_bf{b}", align_bytes=64)
+            z_dst = z_bf[:].bitcast(F32).rearrange("p (j u) -> p j u", u=2)
+            z_src = z_bank[:, : 2 * P].rearrange("p (u j) -> p j u", u=2)
+            if "VVVV"[b] == "V":
+                nc.vector.tensor_copy(z_dst, z_src)
+            else:
+                nc.scalar.copy(z_dst, z_src)
+            z_codes = keep.tile([P, P], U32, name=f"z_codes{b}", align_bytes=64)
+            z_scales = keep.tile([P, P], U8, name=f"z_scales{b}", align_bytes=64)
+            nc.vector.quantize_mx(z_codes[:].bitcast(FP8X4), z_scales[:], z_bf[:])
+            bank = out_bank
+            for c in range(BLOCKS):
+                cols = slice(c * P, (c + 1) * P)
+                nc.tensor.matmul_mx(
+                    bank[:, cols],
+                    lhsT=cand_words[:, cols].bitcast(FP8X4),
+                    lhsT_scale=cand_scales[:, cols],
+                    rhs=z_codes[:].bitcast(FP8X4),
+                    rhs_scale=z_scales[:],
+                    start=True,
+                    stop=True,
+                )
+            result = keep.tile([P, S], F32, name=f"result{b}")
+            nc.scalar.activation(result[:], bank[:], ACT.Copy, scale=0.0625)
+            nc.sync.dma_start(
+                out_blocks[:, :, b * P : (b + 1) * P], result[:].rearrange("p (c n) -> p c n", c=BLOCKS)
+            )
+
+        fetches(0)
+        positions = [position(0)]
+        sums = turned_sums(0)
+        fetches(1)
+        positions.append(position(1))
+        fetches(2)
+        positions.extend(position(b) for b in range(2, BLOCKS))
+        for b in range(BLOCKS):
+            z_rows = curve(b, positions[b], sums)
+            if b + 1 < BLOCKS:
+                sums = turned_sums(b + 1)
+            if b + 3 < BLOCKS:
+                fetches(b + 3)
+            score(b, z_rows)

@@ -19,7 +19,7 @@ ALU = mybir.AluOpType
 P = 128
 PACK = 4
 BLOCKS = S // P
-LIST_COLS = P // 16
+SPAN = 2 * P
 SUM_BANKS = 6
 
 
@@ -46,21 +46,23 @@ def tile_picked_catmull_none_p_kernel(
             )
         offs_l = load_list("offs_l", offs)
         two_l = load_list("two_l", two)
-        cand_l = load_list("cand_l", cand)
+        table_words = keep.tile([P, T], U32, align_bytes=64)
         w1_rows = w1.rearrange("(p j) c -> p j c", j=PACK)
         w1_raw = []
         for h in range(2):
-            raw = keep.tile([P, PACK, S // 2], F32, name=f"w1_raw{h}", tag=f"raw{h}")
+            raw = keep.tile([P, PACK, S // 2], F32, name=f"w1_raw{h}")
             nc.sync.dma_start(raw[:], w1_rows[:, :, h * (S // 2) : (h + 1) * (S // 2)])
             w1_raw.append(raw)
-        table_words = keep.tile([P, T], U32, align_bytes=64)
         nc.sync.dma_start(table_words[:].bitcast(I32), x_words[0].rearrange("p n t -> p (n t)").bitcast(I32))
         gains = keep.tile([P, PACK], F32)
         nc.sync.dma_start(gains[:], gs.rearrange("(p t) o -> p (t o)", t=PACK))
+        w2_raw = keep.tile([P, PACK, S], F32)
+        nc.sync.dma_start(w2_raw[:], w2.rearrange("(p j) c -> p j c", j=PACK))
         k1_l = load_list("k1_l", k1)
+        k3_l = load_list("k3_l", k3)
+        cand_l = load_list("cand_l", cand)
         k2_l = load_list("k2_l", k2)
         k0_l = load_list("k0_l", k0)
-        k3_l = load_list("k3_l", k3)
 
         ident = keep.tile([P, P], F32)
         make_identity(nc, ident[:])
@@ -76,25 +78,26 @@ def tile_picked_catmull_none_p_kernel(
             return tile
 
         offs_scales = pick_scales("offs_scales", offs_l)
-        two_scales = pick_scales("two_scales", two_l)
-        cand_scales = pick_scales("cand_scales", cand_l)
         offs_words = pick_words("offs_words", offs_l)
-        two_words = pick_words("two_words", two_l)
-        cand_words = pick_words("cand_words", cand_l)
 
         w1_bf = keep.tile([P, PACK * S], BF16, align_bytes=64)
         w1_dst = w1_bf[:].rearrange("p (t m j) -> p m j t", t=PACK, j=PACK)
+        w1_src = [raw[:].rearrange("p j (m t) -> p m j t", t=PACK) for raw in w1_raw]
         half = P // 2
-        for h in range(2):
-            nc.scalar.activation(
-                w1_dst[:, h * half : (h + 1) * half], w1_raw[h][:].rearrange("p j (m t) -> p m j t", t=PACK), ACT.Copy
-            )
+        share = 64
+        nc.scalar.activation(w1_dst[:, :half], w1_src[0], ACT.Copy)
+        if share:
+            nc.scalar.activation(w1_dst[:, half : half + share], w1_src[1][:, :share], ACT.Copy)
+        if share < half:
+            nc.vector.tensor_copy(w1_dst[:, half + share :], w1_src[1][:, share:])
         w1_codes = keep.tile([P, S], U32, align_bytes=64)
         w1_scales = keep.tile([P, S], U8, align_bytes=64)
-        nc.vector.quantize_mx(w1_codes[:].bitcast(FP8X4), w1_scales[:], w1_bf[:])
         knots = []
         for t in range(PACK):
             cols = slice(t * P, (t + 1) * P)
+            nc.vector.quantize_mx(
+                w1_codes[:, cols].bitcast(FP8X4), w1_scales[:, cols], w1_bf[:, t * PACK * P : (t + 1) * PACK * P]
+            )
             nc.tensor.matmul_mx(
                 banks[t][:],
                 lhsT=w1_codes[:, cols].bitcast(FP8X4),
@@ -108,74 +111,71 @@ def tile_picked_catmull_none_p_kernel(
             nc.scalar.activation(y[:], banks[t][:], ACT.Copy, scale=gains[:, t : t + 1])
             knots.append(y)
 
-        w2_raw = keep.tile([P, PACK, S], F32, tag="raw1")
-        nc.scalar.dma_start(w2_raw[:], w2.rearrange("(p j) c -> p j c", j=PACK))
-        w2_bf = keep.tile([P, PACK * S], BF16, align_bytes=64, tag="w2_bf")
+        two_scales = pick_scales("two_scales", two_l)
+        two_words = pick_words("two_words", two_l)
+        w2_bf = keep.tile([P, PACK * S], BF16, align_bytes=64)
         w2_dst = w2_bf[:].rearrange("p (c j) -> p c j", j=PACK)
         w2_src = w2_raw[:].rearrange("p j c -> p c j")
-        nc.gpsimd.tensor_scalar(w2_dst, w2_src, 1.0, 0.0, ALU.mult, ALU.add)
-        w2_codes = keep.tile([P, S], U32, align_bytes=64)
+        nc.vector.tensor_copy(w2_dst, w2_src)
+        w2_codes = keep.tile([P, S], U32, align_bytes=64, tag="w2_then_late")
         w2_scales = keep.tile([P, S], U8, align_bytes=64)
         nc.vector.quantize_mx(w2_codes[:].bitcast(FP8X4), w2_scales[:], w2_bf[:])
+        cand_scales = pick_scales("cand_scales", cand_l)
+        cand_words = pick_words("cand_words", cand_l)
 
         fetched = {}
-        negated = [
-            keep.tile([P, 2 * S], F32, name="negated0"),
-            keep.tile([P, 2 * S], F32, name="negated1", align_bytes=64, tag="w2_bf"),
-        ]
-        raw = {name: keep.tile([P, S], F32, name=name) for name in ("slope_raw", "a_slope_raw")}
+        wide_cols = PACK * SPAN
+        late_names = []
 
-        def window(t, lst, b):
-            return knots[t][:].indirect(lst[:, b * LIST_COLS : (b + 1) * LIST_COLS])
+        def window(t, lst, h):
+            return knots[t][:].indirect(lst[:, h * SPAN // 16 : (h + 1) * SPAN // 16])
 
-        def new_tile(name, b):
-            if name == "neg_b":
-                tile = negated[b % 2][:, :S]
-            elif name == "neg_d":
-                tile = negated[b % 2][:, S:]
-            elif name in raw:
-                tile = raw[name][:]
+        def new_tile(name, h, tag):
+            if tag == "late":
+                n = len(late_names)
+                late_names.append(name)
+                tile = late[:, n * wide_cols : (n + 1) * wide_cols]
+            elif tag:
+                tile = keep.tile([P, wide_cols], F32, name=f"{name}{h}", tag=tag)[:]
             else:
-                tile = keep.tile([P, S], F32, name=f"{name}{b}")[:]
-            fetched[name, b] = tile
+                tile = keep.tile([P, wide_cols], F32, name=f"{name}{h}")[:]
+            fetched[name, h] = tile
             return tile
 
-        def fetch(name, lst, b, engine, sign):
-            tile = new_tile(name, b)
+        def part(name, h, t):
+            return fetched[name, h][:, t * SPAN : (t + 1) * SPAN]
+
+        def fetch(name, lst, h, sign, modes="SSSS"):
+            if "S" not in modes:
+                return
+            new_tile(name, h, "late" if h == 1 else None)
             for t in range(PACK):
-                dst = tile[:, t * P : (t + 1) * P]
-                if engine == "S":
-                    nc.scalar.activation(dst, window(t, lst, b), ACT.Copy, scale=sign)
-                elif sign == 1.0:
-                    nc.vector.tensor_copy(dst, window(t, lst, b))
+                if modes[t] == "S":
+                    nc.scalar.activation(part(name, h, t), window(t, lst, h), ACT.Copy, scale=sign)
+
+        def add_to(name, raw, lst, h, other, modes, tag, adder):
+            new_tile(name, h, tag)
+            for t in range(PACK):
+                if modes[t] == "F":
+                    nc.vector.tensor_tensor(part(name, h, t), window(t, lst, h), part(other, h, t), ALU.add)
                 else:
-                    nc.vector.tensor_scalar(dst, window(t, lst, b), sign, 0.0, ALU.mult, ALU.add)
+                    adder.tensor_tensor(part(name, h, t), part(raw, h, t), part(other, h, t), ALU.add)
 
-        def fetch_added(name, lst, b, other, how):
-            if how == "F":
-                tile = new_tile(name, b)
-                for t in range(PACK):
-                    cols = slice(t * P, (t + 1) * P)
-                    nc.vector.tensor_tensor(tile[:, cols], window(t, lst, b), fetched[other, b][:, cols], ALU.add)
-            else:
-                fetch(name + "_raw", lst, b, how, 1.0)
-                tile = new_tile(name, b)
-                nc.gpsimd.tensor_tensor(tile[:], fetched[name + "_raw", b][:], fetched[other, b][:], ALU.add)
-
-        def fetches(b):
-            fetch("neg_b", k1_l, b, "SSSS"[b], -1.0)
-            fetch_added("slope", k2_l, b, "neg_b", "VVVS"[b])
-            fetch_added("a_slope", k0_l, b, "slope", "VVSS"[b])
-            fetch("neg_d", k3_l, b, "SSSS"[b], -1.0)
+        def widen(h, tag, other="knot_a", times=3.0):
+            new_tile("wide", h, tag)
+            for t in range(PACK):
+                nc.vector.scalar_tensor_tensor(
+                    part("wide", h, t), part("slope", h, t), times, part(other, h, t), ALU.mult, ALU.add
+                )
 
         def turn_sum(bank, b, terms):
+            h, first = divmod(b * P, SPAN)
             last = (len(terms) - 1, PACK - 1)
             for n, term in enumerate(terms):
                 for t in range(PACK):
-                    cols = slice(t * P, (t + 1) * P)
                     nc.tensor.matmul(
-                        bank[:, cols],
-                        lhsT=fetched[term, b][:, cols],
+                        bank[:, t * P : (t + 1) * P],
+                        lhsT=fetched[term, h][:, t * SPAN + first : t * SPAN + first + P],
                         rhs=ident[:],
                         start=((n, t) == (0, 0)),
                         stop=((n, t) == last),
@@ -185,9 +185,9 @@ def tile_picked_catmull_none_p_kernel(
 
         def position(b):
             cols = slice(b * P, (b + 1) * P)
-            pos_bank = banks[4 + b]
+            bank = banks[4 + b]
             nc.tensor.matmul_mx(
-                pos_bank[:],
+                bank[:],
                 lhsT=two_words[:, cols].bitcast(FP8X4),
                 lhsT_scale=two_scales[:, cols],
                 rhs=w2_codes[:].bitcast(FP8X4),
@@ -196,13 +196,17 @@ def tile_picked_catmull_none_p_kernel(
                 stop=True,
             )
             pos = keep.tile([P, S], F32, name=f"pos{b}")
-            nc.scalar.activation(pos[:], pos_bank[:], ACT.Sigmoid)
+            nc.scalar.activation(pos[:], bank[:], ACT.Sigmoid)
             return pos
 
         def turned_sums(b):
             sums = [banks[(4 * b + n) % SUM_BANKS] for n in range(4)]
-            cubic = turn_sum(sums[0], b, ["neg_d", "slope", "slope", "a_slope"] if b + 1 < BLOCKS else ["slope", "slope", "a_slope", "neg_d"])
-            bend = turn_sum(sums[1], b, ["neg_b", "a_slope"])
+            mode = "87"[b // 2]
+            cubic_terms = {"8": ["slope", "slope", "a_slope"], "X": ["slope", "slope", "slope", "knot_a"]}.get(mode, ["wide"])
+            cubic_terms = ["neg_d"] + cubic_terms if "00"[b // 2] == "1" else cubic_terms + ["neg_d"]
+            bend_terms = ["neg_b", "slope", "knot_a"] if mode in "7X" else ["neg_b", "a_slope"]
+            cubic = turn_sum(sums[0], b, cubic_terms)
+            bend = turn_sum(sums[1], b, bend_terms)
             slope = turn_sum(sums[2], b, ["slope"])
             neg_b = turn_sum(sums[3], b, ["neg_b"])
             return cubic, bend, slope, neg_b
@@ -210,12 +214,13 @@ def tile_picked_catmull_none_p_kernel(
         def curve(b, pos, sums):
             cubic, bend, slope, neg_b = sums
             z_rows = keep.tile([P, S], BF16, name=f"z_rows{b}")
+            scratch = keep.tile([P, wide_cols], F32, name=f"scratch{b}", tag=f"scratch{b}")
             parts = 2
             width = P // parts
             chains = []
             for h in range(parts):
                 rows = slice(h * width, (h + 1) * width)
-                acc = [keep.tile([P, width, PACK], F32, name=f"acc{n}_{h}_{b}") for n in range(2)]
+                acc = [scratch[:, (2 * h + n) * SPAN : (2 * h + n + 1) * SPAN].rearrange("j (p t) -> j p t", t=PACK) for n in range(2)]
                 pos_h = pos[:].rearrange("j (p t) -> j p t", t=PACK)[:, rows]
                 z_h = z_rows[:].rearrange("j (p t) -> j p t", t=PACK)[:, rows]
                 chains.append((rows, acc[0][:], acc[1][:], pos_h, z_h))
@@ -228,7 +233,7 @@ def tile_picked_catmull_none_p_kernel(
             for rows, u, v, pos_h, z_h in chains:
                 nc.vector.tensor_tensor(v, slope[:, rows], u, ALU.subtract)
             for rows, u, v, pos_h, z_h in chains:
-                (nc.gpsimd if "VVVV"[b] == "G" else nc.vector).tensor_tensor(u, v, pos_h, ALU.mult)
+                nc.vector.tensor_tensor(u, v, pos_h, ALU.mult)
             for rows, u, v, pos_h, z_h in chains:
                 nc.vector.tensor_tensor(z_h, u, neg_b[:, rows], ALU.subtract)
             return z_rows
@@ -242,42 +247,54 @@ def tile_picked_catmull_none_p_kernel(
             z_bf = keep.tile([P, PACK * P], BF16, name=f"z_bf{b}", align_bytes=64)
             z_dst = z_bf[:].bitcast(F32).rearrange("p (j u) -> p j u", u=2)
             z_src = z_bank[:, : 2 * P].rearrange("p (u j) -> p j u", u=2)
-            if "VVVV"[b] == "V":
+            if "VVSS"[b] == "V":
                 nc.vector.tensor_copy(z_dst, z_src)
             else:
                 nc.scalar.copy(z_dst, z_src)
             z_codes = keep.tile([P, P], U32, name=f"z_codes{b}", align_bytes=64)
             z_scales = keep.tile([P, P], U8, name=f"z_scales{b}", align_bytes=64)
             nc.vector.quantize_mx(z_codes[:].bitcast(FP8X4), z_scales[:], z_bf[:])
-            bank = out_bank
-            for c in range(BLOCKS):
-                cols = slice(c * P, (c + 1) * P)
-                nc.tensor.matmul_mx(
-                    bank[:, cols],
-                    lhsT=cand_words[:, cols].bitcast(FP8X4),
-                    lhsT_scale=cand_scales[:, cols],
-                    rhs=z_codes[:].bitcast(FP8X4),
-                    rhs_scale=z_scales[:],
-                    start=True,
-                    stop=True,
-                )
+            split = True and b + 1 == BLOCKS
             result = keep.tile([P, S], F32, name=f"result{b}")
-            nc.scalar.activation(result[:], bank[:], ACT.Copy, scale=0.0625)
-            nc.sync.dma_start(
-                out_blocks[:, :, b * P : (b + 1) * P], result[:].rearrange("p (c n) -> p c n", c=BLOCKS)
-            )
+            groups = [(out_bank, 0, 2), (banks[0], 2, 4)] if split else [(out_bank, 0, 4)]
+            for bank, lo, hi in groups:
+                for c in range(lo, hi):
+                    cols = slice(c * P, (c + 1) * P)
+                    nc.tensor.matmul_mx(
+                        bank[:, cols],
+                        lhsT=cand_words[:, cols].bitcast(FP8X4),
+                        lhsT_scale=cand_scales[:, cols],
+                        rhs=z_codes[:].bitcast(FP8X4),
+                        rhs_scale=z_scales[:],
+                        start=True,
+                        stop=True,
+                    )
+                cols = slice(lo * P, hi * P)
+                if lo == 0:
+                    nc.scalar.activation(result[:, cols], bank[:, cols], ACT.Copy, scale=0.0625)
+                else:
+                    nc.vector.tensor_scalar(result[:, cols], bank[:, cols], 0.0625, None, ALU.mult)
+                nc.sync.dma_start(
+                    out_blocks[:, lo:hi, b * P : (b + 1) * P], result[:, cols].rearrange("p (c n) -> p c n", n=P)
+                )
 
-        fetches(0)
-        positions = [position(0)]
+        fetch("neg_b", k1_l, 0, -1.0)
+        positions = [position(b) for b in range(BLOCKS)]
+        late = keep.tile([P, 4 * wide_cols], F32, name="late", align_bytes=64, tag="w2_then_late")
+        fetch("neg_d", k3_l, 0, -1.0)
+        add_to("slope", None, k2_l, 0, "neg_b", "FFFF", None, None)
+        add_to("a_slope", None, k0_l, 0, "slope", "FFFF", None, None)
         sums = turned_sums(0)
-        fetches(1)
-        positions.append(position(1))
-        fetches(2)
-        positions.extend(position(b) for b in range(2, BLOCKS))
+        fetch("neg_b", k1_l, 1, -1.0)
+        fetch("knot_c", k2_l, 1, 1.0, "SSSS")
+        fetch("knot_a", k0_l, 1, 1.0, "SSSS")
+        fetch("neg_d", k3_l, 1, -1.0)
         for b in range(BLOCKS):
             z_rows = curve(b, positions[b], sums)
+            if b == 0:
+                add_to("slope", "knot_c", k2_l, 1, "neg_b", "SSSS", "scratch0", nc.vector)
+            if b == 1:
+                widen(1, "scratch1")
             if b + 1 < BLOCKS:
                 sums = turned_sums(b + 1)
-            if b + 3 < BLOCKS:
-                fetches(b + 3)
             score(b, z_rows)

@@ -40,12 +40,12 @@ def tile_picked_catmull_none_p_kernel(
 
         table_scales = keep.tile([P, T], U8, align_bytes=64)
         nc.gpsimd.memset(table_scales[:].bitcast(I32), 0)
-        for q in range(4):
-            nc.scalar.dma_start(
-                table_scales[32 * q : 32 * q + 4, :].bitcast(I32), x_scales[0, 4 * q : 4 * q + 4, :].bitcast(I32)
-            )
         offs_l = load_list("offs_l", offs)
         two_l = load_list("two_l", two)
+        for q in range(4):
+            nc.sync.dma_start(
+                table_scales[32 * q : 32 * q + 4, :].bitcast(I32), x_scales[0, 4 * q : 4 * q + 4, :].bitcast(I32)
+            )
         table_words = keep.tile([P, T], U32, align_bytes=64)
         w1_rows = w1.rearrange("(p j) c -> p j c", j=PACK)
         w1_raw = []
@@ -53,6 +53,7 @@ def tile_picked_catmull_none_p_kernel(
             raw = keep.tile([P, PACK, S // 2], F32, name=f"w1_raw{h}")
             nc.sync.dma_start(raw[:], w1_rows[:, :, h * (S // 2) : (h + 1) * (S // 2)])
             w1_raw.append(raw)
+        cand_l = load_list("cand_l", cand)
         nc.sync.dma_start(table_words[:].bitcast(I32), x_words[0].rearrange("p n t -> p (n t)").bitcast(I32))
         gains = keep.tile([P, PACK], F32)
         nc.sync.dma_start(gains[:], gs.rearrange("(p t) o -> p (t o)", t=PACK))
@@ -60,7 +61,6 @@ def tile_picked_catmull_none_p_kernel(
         nc.sync.dma_start(w2_raw[:], w2.rearrange("(p j) c -> p j c", j=PACK))
         k1_l = load_list("k1_l", k1)
         k3_l = load_list("k3_l", k3)
-        cand_l = load_list("cand_l", cand)
         k2_l = load_list("k2_l", k2)
         k0_l = load_list("k0_l", k0)
 
@@ -113,15 +113,15 @@ def tile_picked_catmull_none_p_kernel(
 
         two_scales = pick_scales("two_scales", two_l)
         two_words = pick_words("two_words", two_l)
+        cand_scales = pick_scales("cand_scales", cand_l)
+        cand_words = pick_words("cand_words", cand_l)
         w2_bf = keep.tile([P, PACK * S], BF16, align_bytes=64)
-        w2_dst = w2_bf[:].rearrange("p (c j) -> p c j", j=PACK)
-        w2_src = w2_raw[:].rearrange("p j c -> p c j")
+        w2_dst = w2_bf[:].rearrange("p (t m j) -> p m j t", t=PACK, j=PACK)
+        w2_src = w2_raw[:].rearrange("p j (m t) -> p m j t", t=PACK)
         nc.vector.tensor_copy(w2_dst, w2_src)
         w2_codes = keep.tile([P, S], U32, align_bytes=64, tag="w2_then_late")
         w2_scales = keep.tile([P, S], U8, align_bytes=64)
         nc.vector.quantize_mx(w2_codes[:].bitcast(FP8X4), w2_scales[:], w2_bf[:])
-        cand_scales = pick_scales("cand_scales", cand_l)
-        cand_words = pick_words("cand_words", cand_l)
 
         fetched = {}
         wide_cols = PACK * SPAN
@@ -161,12 +161,26 @@ def tile_picked_catmull_none_p_kernel(
                 else:
                     adder.tensor_tensor(part(name, h, t), part(raw, h, t), part(other, h, t), ALU.add)
 
+        def block(name, h, i):
+            return fetched[name, h].rearrange("p (t j) -> p t j", t=PACK)[:, :, i * P : (i + 1) * P]
+
         def widen(h, tag, other="knot_a", times=3.0):
             new_tile("wide", h, tag)
+            if "BB"[h] == "B":
+                for i in range(2):
+                    nc.vector.scalar_tensor_tensor(
+                        block("wide", h, i), block("slope", h, i), times, block(other, h, i), ALU.mult, ALU.add
+                    )
+            else:
+                for t in range(PACK):
+                    nc.vector.scalar_tensor_tensor(
+                        part("wide", h, t), part("slope", h, t), times, part(other, h, t), ALU.mult, ALU.add
+                    )
+
+        def bend_rows(h, tag, adder):
+            new_tile("bend", h, tag)
             for t in range(PACK):
-                nc.vector.scalar_tensor_tensor(
-                    part("wide", h, t), part("slope", h, t), times, part(other, h, t), ALU.mult, ALU.add
-                )
+                adder.tensor_tensor(part("bend", h, t), part("a_slope", h, t), part("neg_b", h, t), ALU.add)
 
         def turn_sum(bank, b, terms):
             h, first = divmod(b * P, SPAN)
@@ -181,11 +195,11 @@ def tile_picked_catmull_none_p_kernel(
                         stop=((n, t) == last),
                         is_transpose=True,
                     )
-            return bank[:].rearrange("j (t p) -> j p t", t=PACK)
+            return bank[:]
 
         def position(b):
             cols = slice(b * P, (b + 1) * P)
-            bank = banks[4 + b]
+            bank = banks[(2, 5, 6, 7)[b]]
             nc.tensor.matmul_mx(
                 bank[:],
                 lhsT=two_words[:, cols].bitcast(FP8X4),
@@ -200,63 +214,62 @@ def tile_picked_catmull_none_p_kernel(
             return pos
 
         def turned_sums(b):
-            sums = [banks[(4 * b + n) % SUM_BANKS] for n in range(4)]
-            mode = "87"[b // 2]
+            sums = [banks[(0, 1, 2, 3, 4, 5)[(3 * b + n) % SUM_BANKS]] for n in range(3)]
+            mode = "67"[b // 2]
             cubic_terms = {"8": ["slope", "slope", "a_slope"], "X": ["slope", "slope", "slope", "knot_a"]}.get(mode, ["wide"])
-            cubic_terms = ["neg_d"] + cubic_terms if "00"[b // 2] == "1" else cubic_terms + ["neg_d"]
-            bend_terms = ["neg_b", "slope", "knot_a"] if mode in "7X" else ["neg_b", "a_slope"]
+            cubic_terms = cubic_terms[:-1] + ["neg_d"] + cubic_terms[-1:] if "10"[b // 2] == "1" else cubic_terms + ["neg_d"]
+            bend_terms = ["neg_b", "slope", "knot_a"] if mode in "7X" else ["bend"] if mode == "5" else ["neg_b", "a_slope"]
             cubic = turn_sum(sums[0], b, cubic_terms)
             bend = turn_sum(sums[1], b, bend_terms)
             slope = turn_sum(sums[2], b, ["slope"])
-            neg_b = turn_sum(sums[3], b, ["neg_b"])
-            return cubic, bend, slope, neg_b
+            return cubic, bend, slope
 
         def curve(b, pos, sums):
-            cubic, bend, slope, neg_b = sums
-            z_rows = keep.tile([P, S], BF16, name=f"z_rows{b}")
+            cubic, bend, slope = sums
             scratch = keep.tile([P, wide_cols], F32, name=f"scratch{b}", tag=f"scratch{b}")
-            parts = 2
-            width = P // parts
-            chains = []
-            for h in range(parts):
-                rows = slice(h * width, (h + 1) * width)
-                acc = [scratch[:, (2 * h + n) * SPAN : (2 * h + n + 1) * SPAN].rearrange("j (p t) -> j p t", t=PACK) for n in range(2)]
-                pos_h = pos[:].rearrange("j (p t) -> j p t", t=PACK)[:, rows]
-                z_h = z_rows[:].rearrange("j (p t) -> j p t", t=PACK)[:, rows]
-                chains.append((rows, acc[0][:], acc[1][:], pos_h, z_h))
-            for rows, u, v, pos_h, z_h in chains:
-                nc.vector.scalar_tensor_tensor(u, cubic[:, rows], 0.5, pos_h, ALU.mult, ALU.mult)
-            for rows, u, v, pos_h, z_h in chains:
-                nc.vector.scalar_tensor_tensor(v, bend[:, rows], -0.5, u, ALU.mult, ALU.add)
-            for rows, u, v, pos_h, z_h in chains:
-                nc.vector.scalar_tensor_tensor(u, pos_h, 1.0, v, ALU.subtract, ALU.mult)
-            for rows, u, v, pos_h, z_h in chains:
-                nc.vector.tensor_tensor(v, slope[:, rows], u, ALU.subtract)
-            for rows, u, v, pos_h, z_h in chains:
-                nc.vector.tensor_tensor(u, v, pos_h, ALU.mult)
-            for rows, u, v, pos_h, z_h in chains:
-                nc.vector.tensor_tensor(z_h, u, neg_b[:, rows], ALU.subtract)
-            return z_rows
+            u, v = scratch[:, :S], scratch[:, S:]
+            parts = [slice(i * S // 2, (i + 1) * S // 2) for i in range(2)]
+            for c in parts:
+                nc.vector.scalar_tensor_tensor(u[:, c], cubic[:, c], 0.5, pos[:, c], ALU.mult, ALU.mult)
+            for c in parts:
+                nc.vector.scalar_tensor_tensor(v[:, c], bend[:, c], -0.5, u[:, c], ALU.mult, ALU.add)
+            for c in parts:
+                nc.vector.scalar_tensor_tensor(u[:, c], pos[:, c], 1.0, v[:, c], ALU.subtract, ALU.mult)
+            for c in parts:
+                nc.vector.tensor_tensor(v[:, c], slope[:, c], u[:, c], ALU.subtract)
+            for c in parts:
+                nc.vector.tensor_tensor(u[:, c], v[:, c], pos[:, c], ALU.mult)
+            return [u]
 
         out_blocks = out.rearrange("(c p) n -> p c n", p=P)
 
         def score(b, z_rows):
-            words = z_rows[:].bitcast(F32)
-            for u in range(2):
-                nc.tensor.transpose(z_bank[:, u * P : (u + 1) * P], words[:, u : 2 * P : 2], ident[:])
+            for n, term in enumerate(z_rows):
+                for t in range(PACK):
+                    cols = slice(t * P, (t + 1) * P)
+                    nc.tensor.matmul(
+                        z_bank[:, cols],
+                        lhsT=term[:, cols],
+                        rhs=ident[:],
+                        start=((n, t) == (0, 0)),
+                        stop=((n, t) == (0, PACK - 1)),
+                        is_transpose=True,
+                    )
             z_bf = keep.tile([P, PACK * P], BF16, name=f"z_bf{b}", align_bytes=64)
-            z_dst = z_bf[:].bitcast(F32).rearrange("p (j u) -> p j u", u=2)
-            z_src = z_bank[:, : 2 * P].rearrange("p (u j) -> p j u", u=2)
-            if "VVSS"[b] == "V":
-                nc.vector.tensor_copy(z_dst, z_src)
-            else:
-                nc.scalar.copy(z_dst, z_src)
+            h, first = divmod(b * P, SPAN)
+            neg_b = fetched["neg_b", h].rearrange("p (t j) -> p t j", t=PACK)[:, :, first : first + P]
+            nc.vector.tensor_tensor(
+                z_bf[:].rearrange("p (q i t) -> p q t i", i=4, t=PACK),
+                z_bank[:].rearrange("p (t q i) -> p q t i", i=4, t=PACK),
+                neg_b.rearrange("p t (q i) -> p q t i", i=4),
+                ALU.subtract,
+            )
             z_codes = keep.tile([P, P], U32, name=f"z_codes{b}", align_bytes=64)
             z_scales = keep.tile([P, P], U8, name=f"z_scales{b}", align_bytes=64)
             nc.vector.quantize_mx(z_codes[:].bitcast(FP8X4), z_scales[:], z_bf[:])
             split = True and b + 1 == BLOCKS
             result = keep.tile([P, S], F32, name=f"result{b}")
-            groups = [(out_bank, 0, 2), (banks[0], 2, 4)] if split else [(out_bank, 0, 4)]
+            groups = [(out_bank, 0, 2), (banks[4], 2, 4)] if split else [(out_bank, 0, 4)]
             for bank, lo, hi in groups:
                 for c in range(lo, hi):
                     cols = slice(c * P, (c + 1) * P)
@@ -282,19 +295,22 @@ def tile_picked_catmull_none_p_kernel(
         positions = [position(b) for b in range(BLOCKS)]
         late = keep.tile([P, 4 * wide_cols], F32, name="late", align_bytes=64, tag="w2_then_late")
         fetch("neg_d", k3_l, 0, -1.0)
-        add_to("slope", None, k2_l, 0, "neg_b", "FFFF", None, None)
-        add_to("a_slope", None, k0_l, 0, "slope", "FFFF", None, None)
+        add_to("slope", "knot_c", k2_l, 0, "neg_b", "FFFF", None, nc.vector)
+        add_to("a_slope", "knot_a", k0_l, 0, "slope", "FFFF", None, nc.vector)
+        widen(0, None, "a_slope", 2.0)
         sums = turned_sums(0)
         fetch("neg_b", k1_l, 1, -1.0)
-        fetch("knot_c", k2_l, 1, 1.0, "SSSS")
+        fetch("knot_c", k2_l, 1, 1.0, "FFSS")
         fetch("knot_a", k0_l, 1, 1.0, "SSSS")
         fetch("neg_d", k3_l, 1, -1.0)
+        pass
         for b in range(BLOCKS):
             z_rows = curve(b, positions[b], sums)
             if b == 0:
-                add_to("slope", "knot_c", k2_l, 1, "neg_b", "SSSS", "scratch0", nc.vector)
+                add_to("slope", "knot_c", k2_l, 1, "neg_b", "FFSS", "scratch0", nc.vector)
+                widen(1, None)
             if b == 1:
-                widen(1, "scratch1")
+                pass
             if b + 1 < BLOCKS:
                 sums = turned_sums(b + 1)
             score(b, z_rows)

@@ -20,7 +20,13 @@ P = 128
 PACK = 4
 BLOCKS = S // P
 SPAN = 2 * P
+WIDE = PACK * SPAN
+GROUP = 16
+CUBIC, BEND, SLOPE = range(3)
 SUM_BANKS = 6
+
+VECTOR_B_TILES = 1
+VECTOR_C_TILES = 2
 
 
 def tile_picked_catmull_none_p_kernel(
@@ -31,10 +37,9 @@ def tile_picked_catmull_none_p_kernel(
         keep = ctx.enter_context(tc.tile_pool(name="keep", bufs=1))
         psum = ctx.enter_context(tc.psum_pool(name="psum", bufs=1))
         banks = [psum.tile([P, S], F32, name=f"bank{n}") for n in range(8)]
-        z_bank, out_bank = banks[SUM_BANKS:]
 
         def load_list(name, src):
-            tile = keep.tile([P, S // 16], U16, name=name)
+            tile = keep.tile([P, S // GROUP], U16, name=name)
             nc.sync.dma_start(tile[:], src)
             return tile
 
@@ -72,24 +77,33 @@ def tile_picked_catmull_none_p_kernel(
             nc.vector.tensor_copy(tile[:], table_scales[:].indirect(lst[:]))
             return tile
 
-        def pick_words(name, lst):
-            tile = keep.tile([P, S], U32, name=name, align_bytes=64)
+        def pick_words(name, lst, tag):
+            tile = keep.tile([P, S], U32, name=name, align_bytes=64, tag=tag)
             nc.vector.tensor_copy(tile[:], table_words[:].indirect(lst[:]))
             return tile
 
+        def product(dst, lhs_words, lhs_scales, rhs_words, rhs_scales):
+            nc.tensor.matmul_mx(
+                dst,
+                lhsT=lhs_words.bitcast(FP8X4),
+                lhsT_scale=lhs_scales,
+                rhs=rhs_words.bitcast(FP8X4),
+                rhs_scale=rhs_scales,
+                start=True,
+                stop=True,
+            )
+
         offs_scales = pick_scales("offs_scales", offs_l)
-        offs_words = pick_words("offs_words", offs_l)
+        offs_words = pick_words("offs_words", offs_l, "offs_words")
 
         w1_bf = keep.tile([P, PACK * S], BF16, align_bytes=64)
         w1_dst = w1_bf[:].rearrange("p (t m j) -> p m j t", t=PACK, j=PACK)
-        w1_src = [raw[:].rearrange("p j (m t) -> p m j t", t=PACK) for raw in w1_raw]
-        half = P // 2
-        share = 64
-        nc.scalar.activation(w1_dst[:, :half], w1_src[0], ACT.Copy)
-        if share:
-            nc.scalar.activation(w1_dst[:, half : half + share], w1_src[1][:, :share], ACT.Copy)
-        if share < half:
-            nc.vector.tensor_copy(w1_dst[:, half + share :], w1_src[1][:, share:])
+        for h in range(2):
+            nc.scalar.activation(
+                w1_dst[:, h * P // 2 : (h + 1) * P // 2],
+                w1_raw[h][:].rearrange("p j (m t) -> p m j t", t=PACK),
+                ACT.Copy,
+            )
         w1_codes = keep.tile([P, S], U32, align_bytes=64)
         w1_scales = keep.tile([P, S], U8, align_bytes=64)
         knots = []
@@ -98,190 +112,131 @@ def tile_picked_catmull_none_p_kernel(
             nc.vector.quantize_mx(
                 w1_codes[:, cols].bitcast(FP8X4), w1_scales[:, cols], w1_bf[:, t * PACK * P : (t + 1) * PACK * P]
             )
-            nc.tensor.matmul_mx(
-                banks[t][:],
-                lhsT=w1_codes[:, cols].bitcast(FP8X4),
-                lhsT_scale=w1_scales[:, cols],
-                rhs=offs_words[:].bitcast(FP8X4),
-                rhs_scale=offs_scales[:],
-                start=True,
-                stop=True,
-            )
+            product(banks[t][:], w1_codes[:, cols], w1_scales[:, cols], offs_words[:], offs_scales[:])
             y = keep.tile([P, S], F32, name=f"knots{t}")
             nc.scalar.activation(y[:], banks[t][:], ACT.Copy, scale=gains[:, t : t + 1])
             knots.append(y)
 
         two_scales = pick_scales("two_scales", two_l)
-        two_words = pick_words("two_words", two_l)
+        two_words = pick_words("two_words", two_l, "two_words")
         cand_scales = pick_scales("cand_scales", cand_l)
-        cand_words = pick_words("cand_words", cand_l)
-        w2_bf = keep.tile([P, PACK * S], BF16, align_bytes=64)
-        w2_dst = w2_bf[:].rearrange("p (t m j) -> p m j t", t=PACK, j=PACK)
-        w2_src = w2_raw[:].rearrange("p j (m t) -> p m j t", t=PACK)
-        nc.vector.tensor_copy(w2_dst, w2_src)
+        w2_bf = keep.tile([P, PACK * S], BF16, align_bytes=64, tag="w2_then_cand")
+        nc.vector.tensor_copy(
+            w2_bf[:].rearrange("p (t m j) -> p m j t", t=PACK, j=PACK),
+            w2_raw[:].rearrange("p j (m t) -> p m j t", t=PACK),
+        )
         w2_codes = keep.tile([P, S], U32, align_bytes=64, tag="w2_then_late")
         w2_scales = keep.tile([P, S], U8, align_bytes=64)
         nc.vector.quantize_mx(w2_codes[:].bitcast(FP8X4), w2_scales[:], w2_bf[:])
 
-        fetched = {}
-        wide_cols = PACK * SPAN
-        late_names = []
+        rows = {}
 
         def window(t, lst, h):
-            return knots[t][:].indirect(lst[:, h * SPAN // 16 : (h + 1) * SPAN // 16])
-
-        def new_tile(name, h, tag):
-            if tag == "late":
-                n = len(late_names)
-                late_names.append(name)
-                tile = late[:, n * wide_cols : (n + 1) * wide_cols]
-            elif tag:
-                tile = keep.tile([P, wide_cols], F32, name=f"{name}{h}", tag=tag)[:]
-            else:
-                tile = keep.tile([P, wide_cols], F32, name=f"{name}{h}")[:]
-            fetched[name, h] = tile
-            return tile
+            return knots[t][:].indirect(lst[:, h * SPAN // GROUP : (h + 1) * SPAN // GROUP])
 
         def part(name, h, t):
-            return fetched[name, h][:, t * SPAN : (t + 1) * SPAN]
+            return rows[name, h][:, t * SPAN : (t + 1) * SPAN]
 
-        def fetch(name, lst, h, sign, modes="SSSS"):
-            if "S" not in modes:
-                return
-            new_tile(name, h, "late" if h == 1 else None)
-            for t in range(PACK):
-                if modes[t] == "S":
-                    nc.scalar.activation(part(name, h, t), window(t, lst, h), ACT.Copy, scale=sign)
-
-        def add_to(name, raw, lst, h, other, modes, tag, adder):
-            new_tile(name, h, tag)
-            for t in range(PACK):
-                if modes[t] == "F":
-                    nc.vector.tensor_tensor(part(name, h, t), window(t, lst, h), part(other, h, t), ALU.add)
-                else:
-                    adder.tensor_tensor(part(name, h, t), part(raw, h, t), part(other, h, t), ALU.add)
-
-        def block(name, h, i):
-            return fetched[name, h].rearrange("p (t j) -> p t j", t=PACK)[:, :, i * P : (i + 1) * P]
-
-        def widen(h, tag, other="knot_a", times=3.0):
-            new_tile("wide", h, tag)
-            if "BB"[h] == "B":
-                for i in range(2):
-                    nc.vector.scalar_tensor_tensor(
-                        block("wide", h, i), block("slope", h, i), times, block(other, h, i), ALU.mult, ALU.add
-                    )
-            else:
-                for t in range(PACK):
-                    nc.vector.scalar_tensor_tensor(
-                        part("wide", h, t), part("slope", h, t), times, part(other, h, t), ALU.mult, ALU.add
-                    )
-
-        def bend_rows(h, tag, adder):
-            new_tile("bend", h, tag)
-            for t in range(PACK):
-                adder.tensor_tensor(part("bend", h, t), part("a_slope", h, t), part("neg_b", h, t), ALU.add)
-
-        def turn_sum(bank, b, terms):
+        def block(name, b):
             h, first = divmod(b * P, SPAN)
-            last = (len(terms) - 1, PACK - 1)
-            for n, term in enumerate(terms):
-                for t in range(PACK):
-                    nc.tensor.matmul(
-                        bank[:, t * P : (t + 1) * P],
-                        lhsT=fetched[term, h][:, t * SPAN + first : t * SPAN + first + P],
-                        rhs=ident[:],
-                        start=((n, t) == (0, 0)),
-                        stop=((n, t) == last),
-                        is_transpose=True,
-                    )
-            return bank[:]
+            return rows[name, h].rearrange("p (t j) -> p t j", t=PACK)[:, :, first : first + P]
+
+        def new_rows(name, h, tag):
+            rows[name, h] = keep.tile([P, WIDE], F32, name=f"{name}{h}", tag=tag)[:]
+
+        def fetch(name, lst, h, sign, tiles):
+            for t in tiles:
+                nc.scalar.activation(part(name, h, t), window(t, lst, h), ACT.Copy, scale=sign)
+
+        def fetch_plus(name, lst, h, other, tiles):
+            for t in tiles:
+                nc.vector.tensor_tensor(part(name, h, t), window(t, lst, h), part(other, h, t), ALU.add)
+
+        terms = {
+            (CUBIC, 0): ["a_3slope", "neg_d"],
+            (BEND, 0): ["neg_b", "a_slope"],
+            (CUBIC, 1): ["a_3slope", "neg_d"],
+            (BEND, 1): ["neg_b", "slope", "a"],
+            (SLOPE, 0): ["slope"],
+            (SLOPE, 1): ["slope"],
+        }
+
+        def sum_bank(b, which):
+            return banks[(3 * b + which) % SUM_BANKS]
+
+        def turn(dst, src, start, stop):
+            nc.tensor.matmul(dst, lhsT=src, rhs=ident[:], start=start, stop=stop, is_transpose=True)
+
+        def turn_term(b, which, name):
+            names = terms[which, b * P // SPAN]
+            for t in range(PACK):
+                turn(
+                    sum_bank(b, which)[:, t * P : (t + 1) * P],
+                    block(name, b)[:, t],
+                    start=(name == names[0] and t == 0),
+                    stop=(name == names[-1] and t == PACK - 1),
+                )
+
+        def turn_sums(b):
+            for which in (CUBIC, BEND, SLOPE):
+                for name in terms[which, b * P // SPAN]:
+                    turn_term(b, which, name)
 
         def position(b):
             cols = slice(b * P, (b + 1) * P)
-            bank = banks[(2, 5, 6, 7)[b]]
-            nc.tensor.matmul_mx(
-                bank[:],
-                lhsT=two_words[:, cols].bitcast(FP8X4),
-                lhsT_scale=two_scales[:, cols],
-                rhs=w2_codes[:].bitcast(FP8X4),
-                rhs_scale=w2_scales[:],
-                start=True,
-                stop=True,
-            )
-            pos = keep.tile([P, S], F32, name=f"pos{b}")
+            bank = sum_bank(b, BEND) if b < 2 else banks[SUM_BANKS + b - 2]
+            product(bank[:], two_words[:, cols], two_scales[:, cols], w2_codes[:], w2_scales[:])
+            pos = keep.tile([P, S], F32, name=f"pos{b}", tag=f"pos{b}")
             nc.scalar.activation(pos[:], bank[:], ACT.Sigmoid)
             return pos
 
-        def turned_sums(b):
-            sums = [banks[(0, 1, 2, 3, 4, 5)[(3 * b + n) % SUM_BANKS]] for n in range(3)]
-            mode = "67"[b // 2]
-            cubic_terms = {"8": ["slope", "slope", "a_slope"], "X": ["slope", "slope", "slope", "knot_a"]}.get(mode, ["wide"])
-            cubic_terms = cubic_terms[:-1] + ["neg_d"] + cubic_terms[-1:] if "10"[b // 2] == "1" else cubic_terms + ["neg_d"]
-            bend_terms = ["neg_b", "slope", "knot_a"] if mode in "7X" else ["bend"] if mode == "5" else ["neg_b", "a_slope"]
-            cubic = turn_sum(sums[0], b, cubic_terms)
-            bend = turn_sum(sums[1], b, bend_terms)
-            slope = turn_sum(sums[2], b, ["slope"])
-            return cubic, bend, slope
-
-        def curve(b, pos, sums):
-            cubic, bend, slope = sums
-            scratch = keep.tile([P, wide_cols], F32, name=f"scratch{b}", tag=f"scratch{b}")
+        def curve(b):
+            pos = positions[b]
+            scratch = keep.tile([P, 2 * S], F32, name=f"scratch{b}")
             u, v = scratch[:, :S], scratch[:, S:]
-            parts = [slice(i * S // 2, (i + 1) * S // 2) for i in range(2)]
-            for c in parts:
-                nc.vector.scalar_tensor_tensor(u[:, c], cubic[:, c], 0.5, pos[:, c], ALU.mult, ALU.mult)
-            for c in parts:
-                nc.vector.scalar_tensor_tensor(v[:, c], bend[:, c], -0.5, u[:, c], ALU.mult, ALU.add)
-            for c in parts:
+            halves = [slice(0, S // 2), slice(S // 2, S)]
+            for c in halves:
+                nc.vector.scalar_tensor_tensor(u[:, c], sum_bank(b, CUBIC)[:, c], 0.5, pos[:, c], ALU.mult, ALU.mult)
+            for c in halves:
+                nc.vector.scalar_tensor_tensor(v[:, c], sum_bank(b, BEND)[:, c], -0.5, u[:, c], ALU.mult, ALU.add)
+            for c in halves:
                 nc.vector.scalar_tensor_tensor(u[:, c], pos[:, c], 1.0, v[:, c], ALU.subtract, ALU.mult)
-            for c in parts:
-                nc.vector.tensor_tensor(v[:, c], slope[:, c], u[:, c], ALU.subtract)
-            for c in parts:
+            for c in halves:
+                nc.vector.tensor_tensor(v[:, c], sum_bank(b, SLOPE)[:, c], u[:, c], ALU.subtract)
+            for c in halves:
                 nc.vector.tensor_tensor(u[:, c], v[:, c], pos[:, c], ALU.mult)
-            return [u]
+            return u
+
+        def back_bank(b):
+            return banks[SUM_BANKS] if b < 2 else banks[b - 2]
+
+        def turn_back(b, rise):
+            for t in range(PACK):
+                cols = slice(t * P, (t + 1) * P)
+                turn(back_bank(b)[:, cols], rise[:, cols], start=(t == 0), stop=(t == PACK - 1))
 
         out_blocks = out.rearrange("(c p) n -> p c n", p=P)
 
-        def score(b, z_rows):
-            for n, term in enumerate(z_rows):
-                for t in range(PACK):
-                    cols = slice(t * P, (t + 1) * P)
-                    nc.tensor.matmul(
-                        z_bank[:, cols],
-                        lhsT=term[:, cols],
-                        rhs=ident[:],
-                        start=((n, t) == (0, 0)),
-                        stop=((n, t) == (0, PACK - 1)),
-                        is_transpose=True,
-                    )
+        def score(b):
             z_bf = keep.tile([P, PACK * P], BF16, name=f"z_bf{b}", align_bytes=64)
-            h, first = divmod(b * P, SPAN)
-            neg_b = fetched["neg_b", h].rearrange("p (t j) -> p t j", t=PACK)[:, :, first : first + P]
             nc.vector.tensor_tensor(
                 z_bf[:].rearrange("p (q i t) -> p q t i", i=4, t=PACK),
-                z_bank[:].rearrange("p (t q i) -> p q t i", i=4, t=PACK),
-                neg_b.rearrange("p t (q i) -> p q t i", i=4),
+                back_bank(b)[:].rearrange("p (t q i) -> p q t i", i=4, t=PACK),
+                block("neg_b", b).rearrange("p t (q i) -> p q t i", i=4),
                 ALU.subtract,
             )
             z_codes = keep.tile([P, P], U32, name=f"z_codes{b}", align_bytes=64)
             z_scales = keep.tile([P, P], U8, name=f"z_scales{b}", align_bytes=64)
             nc.vector.quantize_mx(z_codes[:].bitcast(FP8X4), z_scales[:], z_bf[:])
-            split = True and b + 1 == BLOCKS
             result = keep.tile([P, S], F32, name=f"result{b}")
-            groups = [(out_bank, 0, 2), (banks[4], 2, 4)] if split else [(out_bank, 0, 4)]
-            for bank, lo, hi in groups:
+            if b + 1 < BLOCKS:
+                shares = [(banks[SUM_BANKS + 1], 0, BLOCKS)]
+            else:
+                shares = [(banks[3], 0, BLOCKS // 2), (banks[2], BLOCKS // 2, BLOCKS)]
+            for bank, lo, hi in shares:
                 for c in range(lo, hi):
                     cols = slice(c * P, (c + 1) * P)
-                    nc.tensor.matmul_mx(
-                        bank[:, cols],
-                        lhsT=cand_words[:, cols].bitcast(FP8X4),
-                        lhsT_scale=cand_scales[:, cols],
-                        rhs=z_codes[:].bitcast(FP8X4),
-                        rhs_scale=z_scales[:],
-                        start=True,
-                        stop=True,
-                    )
+                    product(bank[:, cols], cand_words[:, cols], cand_scales[:, cols], z_codes[:], z_scales[:])
                 cols = slice(lo * P, hi * P)
                 if lo == 0:
                     nc.scalar.activation(result[:, cols], bank[:, cols], ACT.Copy, scale=0.0625)
@@ -291,26 +246,58 @@ def tile_picked_catmull_none_p_kernel(
                     out_blocks[:, lo:hi, b * P : (b + 1) * P], result[:, cols].rearrange("p (c n) -> p c n", n=P)
                 )
 
-        fetch("neg_b", k1_l, 0, -1.0)
+        every = range(PACK)
+        new_rows("neg_b", 0, "neg_b0")
+        for t in range(VECTOR_B_TILES):
+            nc.vector.tensor_scalar(part("neg_b", 0, t), window(t, k1_l, 0), -1.0, 0.0, ALU.mult, ALU.add)
+        fetch("neg_b", k1_l, 0, -1.0, range(VECTOR_B_TILES, PACK))
         positions = [position(b) for b in range(BLOCKS)]
-        late = keep.tile([P, 4 * wide_cols], F32, name="late", align_bytes=64, tag="w2_then_late")
-        fetch("neg_d", k3_l, 0, -1.0)
-        add_to("slope", "knot_c", k2_l, 0, "neg_b", "FFFF", None, nc.vector)
-        add_to("a_slope", "knot_a", k0_l, 0, "slope", "FFFF", None, nc.vector)
-        widen(0, None, "a_slope", 2.0)
-        sums = turned_sums(0)
-        fetch("neg_b", k1_l, 1, -1.0)
-        fetch("knot_c", k2_l, 1, 1.0, "FFSS")
-        fetch("knot_a", k0_l, 1, 1.0, "SSSS")
-        fetch("neg_d", k3_l, 1, -1.0)
-        pass
-        for b in range(BLOCKS):
-            z_rows = curve(b, positions[b], sums)
-            if b == 0:
-                add_to("slope", "knot_c", k2_l, 1, "neg_b", "FFSS", "scratch0", nc.vector)
-                widen(1, None)
-            if b == 1:
-                pass
-            if b + 1 < BLOCKS:
-                sums = turned_sums(b + 1)
-            score(b, z_rows)
+        late_rows = [("neg_d", 0), ("neg_b", 1), ("c", 1), ("a", 1), ("neg_d", 1)]
+        late = keep.tile([P, len(late_rows) * WIDE], F32, align_bytes=64, tag="w2_then_late")
+        for n, key in enumerate(late_rows):
+            rows[key] = late[:, n * WIDE : (n + 1) * WIDE]
+        fetch("neg_d", k3_l, 0, -1.0, every)
+        new_rows("slope", 0, "slope0")
+        fetch_plus("slope", k2_l, 0, "neg_b", every)
+        new_rows("a_slope", 0, "a_slope0")
+        fetch_plus("a_slope", k0_l, 0, "slope", every)
+        new_rows("a_3slope", 0, "a_3slope0")
+        for t in every:
+            nc.vector.scalar_tensor_tensor(
+                part("a_3slope", 0, t), part("slope", 0, t), 2.0, part("a_slope", 0, t), ALU.mult, ALU.add
+            )
+        cand_words = pick_words("cand_words", cand_l, "w2_then_cand")
+        turn_term(0, BEND, "neg_b")
+        turn_term(1, BEND, "neg_b")
+        turn_term(0, SLOPE, "slope")
+        turn_term(0, BEND, "a_slope")
+        for b in range(2):
+            turn_term(b, CUBIC, "a_3slope")
+            turn_term(b, CUBIC, "neg_d")
+        turn_term(1, BEND, "a_slope")
+        turn_term(1, SLOPE, "slope")
+
+        fetch("neg_b", k1_l, 1, -1.0, every)
+        fetch("c", k2_l, 1, 1.0, range(VECTOR_C_TILES, PACK))
+        fetch("a", k0_l, 1, 1.0, every)
+        fetch("neg_d", k3_l, 1, -1.0, every)
+        rise = curve(0)
+        new_rows("slope", 1, "pos0")
+        fetch_plus("slope", k2_l, 1, "neg_b", range(VECTOR_C_TILES))
+        for t in range(VECTOR_C_TILES, PACK):
+            nc.vector.tensor_tensor(part("slope", 1, t), part("c", 1, t), part("neg_b", 1, t), ALU.add)
+        new_rows("a_3slope", 1, "a_3slope1")
+        for b in range(2, BLOCKS):
+            nc.vector.scalar_tensor_tensor(
+                block("a_3slope", b), block("slope", b), 3.0, block("a", b), ALU.mult, ALU.add
+            )
+        turn_back(0, rise)
+        score(0)
+        turn_sums(2)
+        turn_back(1, curve(1))
+        turn_sums(3)
+        for b in range(2, BLOCKS):
+            rise = curve(b)
+            score(b - 1)
+            turn_back(b, rise)
+        score(BLOCKS - 1)

@@ -69,6 +69,8 @@ def tile_picked_catmull_none_p_kernel(
         k2_l = load_list("k2_l", k2)
         k0_l = load_list("k0_l", k0)
 
+        minus_half = keep.tile([P, 1], F32)
+        nc.gpsimd.memset(minus_half[:], -0.5)
         ident = keep.tile([P, P], F32)
         make_identity(nc, ident[:])
 
@@ -190,11 +192,12 @@ def tile_picked_catmull_none_p_kernel(
             nc.scalar.activation(pos[:], bank[:], ACT.Sigmoid)
             return pos
 
-        def curve(b):
+        halves = [slice(0, S // 2), slice(S // 2, S)]
+
+        def curve_nested(b):
             pos = positions[b]
             scratch = keep.tile([P, 2 * S], F32, name=f"scratch{b}")
             u, v = scratch[:, :S], scratch[:, S:]
-            halves = [slice(0, S // 2), slice(S // 2, S)]
             for c in halves:
                 nc.vector.scalar_tensor_tensor(u[:, c], sum_bank(b, CUBIC)[:, c], 0.5, pos[:, c], ALU.mult, ALU.mult)
             for c in halves:
@@ -205,15 +208,39 @@ def tile_picked_catmull_none_p_kernel(
                 nc.vector.tensor_tensor(v[:, c], sum_bank(b, SLOPE)[:, c], u[:, c], ALU.subtract)
             for c in halves:
                 nc.vector.tensor_tensor(u[:, c], v[:, c], pos[:, c], ALU.mult)
-            return u
+            return [u]
+
+        def square(b):
+            tile = keep.tile([P, S], F32, name=f"square{b}")
+            nc.scalar.activation(tile[:], positions[b][:], ACT.Square, bias=minus_half[:])
+            return tile
+
+        def curve_split(b):
+            pos = positions[b]
+            scratch = keep.tile([P, 3 * S], F32, name=f"scratch{b}")
+            u, v, line = scratch[:, :S], scratch[:, S : 2 * S], scratch[:, 2 * S :]
+            for c in halves:
+                nc.vector.scalar_tensor_tensor(u[:, c], sum_bank(b, CUBIC)[:, c], -0.5, pos[:, c], ALU.mult, ALU.mult)
+            for c in halves:
+                nc.vector.scalar_tensor_tensor(v[:, c], sum_bank(b, BEND)[:, c], 0.5, u[:, c], ALU.mult, ALU.add)
+            nc.vector.tensor_tensor(line, sum_bank(b, SLOPE)[:], pos[:], ALU.mult)
+            for c in halves:
+                nc.vector.scalar_tensor_tensor(u[:, c], squares[b][:, c], 0.25, v[:, c], ALU.subtract, ALU.mult)
+            return [line, u]
 
         def back_bank(b):
             return banks[SUM_BANKS] if b < 2 else banks[b - 2]
 
         def turn_back(b, rise):
-            for t in range(PACK):
-                cols = slice(t * P, (t + 1) * P)
-                turn(back_bank(b)[:, cols], rise[:, cols], start=(t == 0), stop=(t == PACK - 1))
+            for n, tile in enumerate(rise):
+                for t in range(PACK):
+                    cols = slice(t * P, (t + 1) * P)
+                    turn(
+                        back_bank(b)[:, cols],
+                        tile[:, cols],
+                        start=(n == 0 and t == 0),
+                        stop=(n == len(rise) - 1 and t == PACK - 1),
+                    )
 
         out_blocks = out.rearrange("(c p) n -> p c n", p=P)
 
@@ -281,7 +308,8 @@ def tile_picked_catmull_none_p_kernel(
         fetch("c", k2_l, 1, 1.0, range(VECTOR_C_TILES, PACK))
         fetch("a", k0_l, 1, 1.0, every)
         fetch("neg_d", k3_l, 1, -1.0, every)
-        rise = curve(0)
+        squares = {b: square(b) for b in range(2, BLOCKS)}
+        rise = curve_nested(0)
         new_rows("slope", 1, "pos0")
         fetch_plus("slope", k2_l, 1, "neg_b", range(VECTOR_C_TILES))
         for t in range(VECTOR_C_TILES, PACK):
@@ -294,10 +322,10 @@ def tile_picked_catmull_none_p_kernel(
         turn_back(0, rise)
         score(0)
         turn_sums(2)
-        turn_back(1, curve(1))
+        turn_back(1, curve_nested(1))
         turn_sums(3)
         for b in range(2, BLOCKS):
-            rise = curve(b)
+            rise = curve_split(b)
             score(b - 1)
             turn_back(b, rise)
         score(BLOCKS - 1)

from contextlib import ExitStack

import concourse.mybir as mybir
from concourse.masks import make_identity

K, T, S = 512, 2048, 512
FLOPS = 3 * 2 * K * S * S

F32 = mybir.dt.float32
BF16 = mybir.dt.bfloat16
I32 = mybir.dt.int32
U32 = mybir.dt.uint32
U16 = mybir.dt.uint16
U8 = mybir.dt.uint8
FP8X4 = mybir.dt.float8_e4m3fn_x4
ACT = mybir.ActivationFunctionType
ALU = mybir.AluOpType

P = 128
PACK = 4
BLOCKS = S // P
SPAN = 2 * P
WIDE = PACK * SPAN
GROUP = 16
CUBIC, BEND, SLOPE = range(3)
SUM_BANKS = 6

VECTOR_B_TILES = 1
VECTOR_C_TILES = 2


def tile_picked_catmull_none_p_kernel(
    tc, x_words, x_scales, w1, w2, gs, offs, two, k0, k1, k2, k3, cand, out
):
    nc = tc.nc
    with ExitStack() as ctx:
        keep = ctx.enter_context(tc.tile_pool(name="keep", bufs=1))
        psum = ctx.enter_context(tc.psum_pool(name="psum", bufs=1))
        banks = [psum.tile([P, S], F32, name=f"bank{n}") for n in range(8)]

        def load_list(name, src):
            tile = keep.tile([P, S // GROUP], U16, name=name)
            nc.sync.dma_start(tile[:], src)
            return tile

        table_scales = keep.tile([P, T], U8, align_bytes=64)
        nc.gpsimd.memset(table_scales[:].bitcast(I32), 0)
        offs_l = load_list("offs_l", offs)
        two_l = load_list("two_l", two)
        for q in range(4):
            nc.sync.dma_start(
                table_scales[32 * q : 32 * q + 4, :].bitcast(I32), x_scales[0, 4 * q : 4 * q + 4, :].bitcast(I32)
            )
        table_words = keep.tile([P, T], U32, align_bytes=64)
        w1_rows = w1.rearrange("(p j) c -> p j c", j=PACK)
        w1_raw = []
        for h in range(2):
            raw = keep.tile([P, PACK, S // 2], F32, name=f"w1_raw{h}")
            nc.sync.dma_start(raw[:], w1_rows[:, :, h * (S // 2) : (h + 1) * (S // 2)])
            w1_raw.append(raw)
        cand_l = load_list("cand_l", cand)
        nc.sync.dma_start(table_words[:].bitcast(I32), x_words[0].rearrange("p n t -> p (n t)").bitcast(I32))
        gains = keep.tile([P, PACK], F32)
        nc.sync.dma_start(gains[:], gs.rearrange("(p t) o -> p (t o)", t=PACK))
        w2_raw = keep.tile([P, PACK, S], F32)
        nc.sync.dma_start(w2_raw[:], w2.rearrange("(p j) c -> p j c", j=PACK))
        k1_l = load_list("k1_l", k1)
        k3_l = load_list("k3_l", k3)
        k2_l = load_list("k2_l", k2)
        k0_l = load_list("k0_l", k0)

        minus_half = keep.tile([P, 1], F32)
        nc.gpsimd.memset(minus_half[:], -0.5)
        ident = keep.tile([P, P], F32)
        make_identity(nc, ident[:])

        def pick_scales(name, lst):
            tile = keep.tile([P, S], U8, name=name, align_bytes=64)
            nc.vector.tensor_copy(tile[:], table_scales[:].indirect(lst[:]))
            return tile

        def pick_words(name, lst, tag):
            tile = keep.tile([P, S], U32, name=name, align_bytes=64, tag=tag)
            nc.vector.tensor_copy(tile[:], table_words[:].indirect(lst[:]))
            return tile

        def product(dst, lhs_words, lhs_scales, rhs_words, rhs_scales):
            nc.tensor.matmul_mx(
                dst,
                lhsT=lhs_words.bitcast(FP8X4),
                lhsT_scale=lhs_scales,
                rhs=rhs_words.bitcast(FP8X4),
                rhs_scale=rhs_scales,
                start=True,
                stop=True,
            )

        offs_scales = pick_scales("offs_scales", offs_l)
        offs_words = pick_words("offs_words", offs_l, "offs_words")

        w1_bf = keep.tile([P, PACK * S], BF16, align_bytes=64)
        w1_dst = w1_bf[:].rearrange("p (t m j) -> p m j t", t=PACK, j=PACK)
        for h in range(2):
            nc.scalar.activation(
                w1_dst[:, h * P // 2 : (h + 1) * P // 2],
                w1_raw[h][:].rearrange("p j (m t) -> p m j t", t=PACK),
                ACT.Copy,
            )
        w1_codes = keep.tile([P, S], U32, align_bytes=64)
        w1_scales = keep.tile([P, S], U8, align_bytes=64)
        knots = []
        for t in range(PACK):
            cols = slice(t * P, (t + 1) * P)
            nc.vector.quantize_mx(
                w1_codes[:, cols].bitcast(FP8X4), w1_scales[:, cols], w1_bf[:, t * PACK * P : (t + 1) * PACK * P]
            )
            product(banks[t][:], w1_codes[:, cols], w1_scales[:, cols], offs_words[:], offs_scales[:])
            y = keep.tile([P, S], F32, name=f"knots{t}")
            nc.scalar.activation(y[:], banks[t][:], ACT.Copy, scale=gains[:, t : t + 1])
            knots.append(y)

        two_scales = pick_scales("two_scales", two_l)
        two_words = pick_words("two_words", two_l, "two_words")
        cand_scales = pick_scales("cand_scales", cand_l)
        w2_bf = keep.tile([P, PACK * S], BF16, align_bytes=64, tag="w2_then_cand")
        nc.vector.tensor_copy(
            w2_bf[:].rearrange("p (t m j) -> p m j t", t=PACK, j=PACK),
            w2_raw[:].rearrange("p j (m t) -> p m j t", t=PACK),
        )
        w2_codes = keep.tile([P, S], U32, align_bytes=64, tag="w2_then_late")
        w2_scales = keep.tile([P, S], U8, align_bytes=64)
        nc.vector.quantize_mx(w2_codes[:].bitcast(FP8X4), w2_scales[:], w2_bf[:])

        rows = {}

        def window(t, lst, h):
            return knots[t][:].indirect(lst[:, h * SPAN // GROUP : (h + 1) * SPAN // GROUP])

        def part(name, h, t):
            return rows[name, h][:, t * SPAN : (t + 1) * SPAN]

        def block(name, b):
            h, first = divmod(b * P, SPAN)
            return rows[name, h].rearrange("p (t j) -> p t j", t=PACK)[:, :, first : first + P]

        def new_rows(name, h, tag):
            rows[name, h] = keep.tile([P, WIDE], F32, name=f"{name}{h}", tag=tag)[:]

        def fetch(name, lst, h, sign, tiles):
            for t in tiles:
                nc.scalar.activation(part(name, h, t), window(t, lst, h), ACT.Copy, scale=sign)

        def fetch_plus(name, lst, h, other, tiles):
            for t in tiles:
                nc.vector.tensor_tensor(part(name, h, t), window(t, lst, h), part(other, h, t), ALU.add)

        terms = {
            (CUBIC, 0): ["a_3slope", "neg_d"],
            (BEND, 0): ["neg_b", "a_slope"],
            (CUBIC, 1): ["a_3slope", "neg_d"],
            (BEND, 1): ["neg_b", "slope", "a"],
            (SLOPE, 0): ["slope"],
            (SLOPE, 1): ["slope"],
        }

        def sum_bank(b, which):
            return banks[(3 * b + which) % SUM_BANKS]

        def turn(dst, src, start, stop):
            nc.tensor.matmul(dst, lhsT=src, rhs=ident[:], start=start, stop=stop, is_transpose=True)

        def turn_term(b, which, name):
            names = terms[which, b * P // SPAN]
            for t in range(PACK):
                turn(
                    sum_bank(b, which)[:, t * P : (t + 1) * P],
                    block(name, b)[:, t],
                    start=(name == names[0] and t == 0),
                    stop=(name == names[-1] and t == PACK - 1),
                )

        def turn_sums(b):
            for which in (CUBIC, BEND, SLOPE):
                for name in terms[which, b * P // SPAN]:
                    turn_term(b, which, name)

        def position(b):
            cols = slice(b * P, (b + 1) * P)
            bank = sum_bank(b, BEND) if b < 2 else banks[SUM_BANKS + b - 2]
            product(bank[:], two_words[:, cols], two_scales[:, cols], w2_codes[:], w2_scales[:])
            pos = keep.tile([P, S], F32, name=f"pos{b}", tag=f"pos{b}")
            nc.scalar.activation(pos[:], bank[:], ACT.Sigmoid)
            return pos

        halves = [slice(0, S // 2), slice(S // 2, S)]

        def curve_nested(b):
            pos = positions[b]
            scratch = keep.tile([P, 2 * S], F32, name=f"scratch{b}")
            u, v = scratch[:, :S], scratch[:, S:]
            for c in halves:
                nc.vector.scalar_tensor_tensor(u[:, c], sum_bank(b, CUBIC)[:, c], 0.5, pos[:, c], ALU.mult, ALU.mult)
            for c in halves:
                nc.vector.scalar_tensor_tensor(v[:, c], sum_bank(b, BEND)[:, c], -0.5, u[:, c], ALU.mult, ALU.add)
            for c in halves:
                nc.vector.scalar_tensor_tensor(u[:, c], pos[:, c], 1.0, v[:, c], ALU.subtract, ALU.mult)
            for c in halves:
                nc.vector.tensor_tensor(v[:, c], sum_bank(b, SLOPE)[:, c], u[:, c], ALU.subtract)
            for c in halves:
                nc.vector.tensor_tensor(u[:, c], v[:, c], pos[:, c], ALU.mult)
            return [u]

        def square(b):
            tile = keep.tile([P, S], F32, name=f"square{b}")
            nc.scalar.activation(tile[:], positions[b][:], ACT.Square, bias=minus_half[:])
            return tile

        def curve_split(b):
            pos = positions[b]
            scratch = keep.tile([P, 3 * S], F32, name=f"scratch{b}")
            u, v, line = scratch[:, :S], scratch[:, S : 2 * S], scratch[:, 2 * S :]
            for c in halves:
                nc.vector.scalar_tensor_tensor(u[:, c], sum_bank(b, CUBIC)[:, c], -0.5, pos[:, c], ALU.mult, ALU.mult)
            for c in halves:
                nc.vector.scalar_tensor_tensor(v[:, c], sum_bank(b, BEND)[:, c], 0.5, u[:, c], ALU.mult, ALU.add)
            nc.vector.tensor_tensor(line, sum_bank(b, SLOPE)[:], pos[:], ALU.mult)
            for c in halves:
                nc.vector.scalar_tensor_tensor(u[:, c], squares[b][:, c], 0.25, v[:, c], ALU.subtract, ALU.mult)
            return [line, u]

        def back_bank(b):
            return banks[SUM_BANKS] if b < 2 else banks[b - 2]

        def turn_back(b, rise):
            for n, tile in enumerate(rise):
                for t in range(PACK):
                    cols = slice(t * P, (t + 1) * P)
                    turn(
                        back_bank(b)[:, cols],
                        tile[:, cols],
                        start=(n == 0 and t == 0),
                        stop=(n == len(rise) - 1 and t == PACK - 1),
                    )

        out_blocks = out.rearrange("(c p) n -> p c n", p=P)

        def score(b):
            z_bf = keep.tile([P, PACK * P], BF16, name=f"z_bf{b}", align_bytes=64)
            nc.vector.tensor_tensor(
                z_bf[:].rearrange("p (q i t) -> p q t i", i=4, t=PACK),
                back_bank(b)[:].rearrange("p (t q i) -> p q t i", i=4, t=PACK),
                block("neg_b", b).rearrange("p t (q i) -> p q t i", i=4),
                ALU.subtract,
            )
            z_codes = keep.tile([P, P], U32, name=f"z_codes{b}", align_bytes=64)
            z_scales = keep.tile([P, P], U8, name=f"z_scales{b}", align_bytes=64)
            nc.vector.quantize_mx(z_codes[:].bitcast(FP8X4), z_scales[:], z_bf[:])
            result = keep.tile([P, S], F32, name=f"result{b}")
            if b + 1 < BLOCKS:
                shares = [(banks[SUM_BANKS + 1], 0, BLOCKS)]
            else:
                shares = [(banks[3], 0, BLOCKS // 2), (banks[2], BLOCKS // 2, BLOCKS)]
            for bank, lo, hi in shares:
                for c in range(lo, hi):
                    cols = slice(c * P, (c + 1) * P)
                    product(bank[:, cols], cand_words[:, cols], cand_scales[:, cols], z_codes[:], z_scales[:])
                cols = slice(lo * P, hi * P)
                if lo == 0:
                    nc.scalar.activation(result[:, cols], bank[:, cols], ACT.Copy, scale=0.0625)
                else:
                    nc.vector.tensor_scalar(result[:, cols], bank[:, cols], 0.0625, None, ALU.mult)
                nc.sync.dma_start(
                    out_blocks[:, lo:hi, b * P : (b + 1) * P], result[:, cols].rearrange("p (c n) -> p c n", n=P)
                )

        every = range(PACK)
        new_rows("neg_b", 0, "neg_b0")
        for t in range(VECTOR_B_TILES):
            nc.vector.tensor_scalar(part("neg_b", 0, t), window(t, k1_l, 0), -1.0, 0.0, ALU.mult, ALU.add)
        fetch("neg_b", k1_l, 0, -1.0, range(VECTOR_B_TILES, PACK))
        positions = [position(b) for b in range(BLOCKS)]
        late_rows = [("neg_d", 0), ("neg_b", 1), ("c", 1), ("a", 1), ("neg_d", 1)]
        late = keep.tile([P, len(late_rows) * WIDE], F32, align_bytes=64, tag="w2_then_late")
        for n, key in enumerate(late_rows):
            rows[key] = late[:, n * WIDE : (n + 1) * WIDE]
        fetch("neg_d", k3_l, 0, -1.0, every)
        new_rows("slope", 0, "slope0")
        fetch_plus("slope", k2_l, 0, "neg_b", every)
        new_rows("a_slope", 0, "a_slope0")
        fetch_plus("a_slope", k0_l, 0, "slope", every)
        new_rows("a_3slope", 0, "a_3slope0")
        for t in every:
            nc.vector.scalar_tensor_tensor(
                part("a_3slope", 0, t), part("slope", 0, t), 2.0, part("a_slope", 0, t), ALU.mult, ALU.add
            )
        cand_words = pick_words("cand_words", cand_l, "w2_then_cand")
        turn_term(0, BEND, "neg_b")
        turn_term(1, BEND, "neg_b")
        turn_term(0, SLOPE, "slope")
        turn_term(0, BEND, "a_slope")
        for b in range(2):
            turn_term(b, CUBIC, "a_3slope")
            turn_term(b, CUBIC, "neg_d")
        turn_term(1, BEND, "a_slope")
        turn_term(1, SLOPE, "slope")

        fetch("neg_b", k1_l, 1, -1.0, every)
        fetch("c", k2_l, 1, 1.0, range(VECTOR_C_TILES, PACK))
        fetch("a", k0_l, 1, 1.0, every)
        fetch("neg_d", k3_l, 1, -1.0, every)
        squares = {b: square(b) for b in range(2, BLOCKS)}
        rise = curve_nested(0)
        new_rows("slope", 1, "pos0")
        fetch_plus("slope", k2_l, 1, "neg_b", range(VECTOR_C_TILES))
        for t in range(VECTOR_C_TILES, PACK):
            nc.vector.tensor_tensor(part("slope", 1, t), part("c", 1, t), part("neg_b", 1, t), ALU.add)
        new_rows("a_3slope", 1, "a_3slope1")
        for b in range(2, BLOCKS):
            nc.vector.scalar_tensor_tensor(
                block("a_3slope", b), block("slope", b), 3.0, block("a", b), ALU.mult, ALU.add
            )
        turn_back(0, rise)
        score(0)
        turn_sums(2)
        turn_back(1, curve_nested(1))
        turn_sums(3)
        for b in range(2, BLOCKS):
            rise = curve_split(b)
            score(b - 1)
            turn_back(b, rise)
        score(BLOCKS - 1)
